import numpy as np
import ml_dtypes


def mxq(x, axis, fmt="e4m3"):
    dtype, down = {"e4m3": (ml_dtypes.float8_e4m3fn, 7), "e5m2": (ml_dtypes.float8_e5m2, 14)}[fmt]
    v = np.moveaxis(np.asarray(x, np.float32).astype(ml_dtypes.bfloat16).astype(np.float64), axis, -1)
    blocks = v.reshape(v.shape[:-1] + (-1, 32))
    amax = np.abs(blocks).max(-1, keepdims=True)
    byte = np.maximum(np.where(amax > 0, np.frexp(amax)[1] - 1 + 127, 0) - down, 1)
    scale = np.exp2(byte - 127.0)
    codes = (blocks / scale).astype(np.float32).astype(dtype).astype(np.float64)
    return np.moveaxis((codes * scale).reshape(v.shape), -1, axis)


WIDE = False


def mx_kscale(k):
    if not WIDE:
        return np.ones(k)
    levels = np.array([10, -10, 5, -5, 0])
    if k % 512:
        return np.exp2(np.random.permutation(np.resize(levels, k // 32))).repeat(32)
    a = np.empty((k // 512, 16))
    for p in range(k // 512):
        a[p, :8] = np.random.permutation(np.resize(levels, 8))
        for g in range(8):
            far = levels[np.abs(levels - a[p, g]) >= 10]
            a[p, g + 8] = far[np.random.randint(len(far))]
    return np.exp2(a.ravel()).repeat(32)


def f64(x):
    return np.asarray(x).astype(np.float64)


def striped(idx):
    return np.tile(idx.reshape(-1, 16).T, (8, 1)).astype(np.uint16)


def unstriped(offs):
    return offs[:16].T.reshape(-1).astype(np.int64)


E2M1 = np.array([0.0, 0.5, 1.0, 1.5, 2.0, 3.0, 4.0, 6.0, -0.0, -0.5, -1.0, -1.5, -2.0, -3.0, -4.0, -6.0])


def pack_weight(w, fmt):
    k, n = w.shape
    w = f64(np.asarray(w, np.float32).astype(ml_dtypes.bfloat16)).reshape(k // 32, 32, n)
    amax = np.abs(w).max(1)
    if fmt == "e4m3":
        byte = np.frexp(amax)[1] - 1 + 127 - 7
    else:
        mant, ex = np.frexp(amax / 6.0)
        byte = np.where(mant > 0.5, ex, ex - 1) + 127
    byte = np.clip(np.where(amax > 0, byte, 1), 1, 254)
    scaled = (w * np.exp2(127.0 - byte)[:, None, :]).reshape(k, n).astype(np.float32)
    by_word = np.ascontiguousarray(scaled.reshape(k // 512, 128, 4, n).transpose(0, 1, 3, 2))
    if fmt == "e4m3":
        words = by_word.astype(ml_dtypes.float8_e4m3fn).view(np.uint8)
    else:
        c = by_word.astype(ml_dtypes.float4_e2m1fn).view(np.uint8) & 0xF
        words = (c[..., 0::2] | (c[..., 1::2] << 4)).reshape(k // 512, 128, 2 * n)
    return np.ascontiguousarray(words), np.ascontiguousarray(byte.astype(np.uint8).reshape(k // 512, 16, n))


def unpack_weight(words, scales, fmt):
    g, _, n = scales.shape
    words = np.ascontiguousarray(words).reshape(g, 128, n, -1)
    if fmt == "e4m3":
        vals = words.view(ml_dtypes.float8_e4m3fn).astype(np.float64)
    else:
        nib = np.empty((g, 128, n, 4), np.uint8)
        nib[..., 0::2] = words & 0xF
        nib[..., 1::2] = words >> 4
        vals = E2M1[nib]
    vals = vals * np.repeat(np.exp2(scales.astype(np.float64) - 127.0), 8, axis=1)[..., None]
    return vals.transpose(0, 1, 3, 2).reshape(g * 512, n)


def gelu(v):
    return 0.5 * v * (1.0 + np.tanh(np.sqrt(2.0 / np.pi) * (v + 0.044715 * v**3)))


K, K2, H, N, T, S, T2 = 1024, 512, 1024, 256, 2048, 1024, 2048

def setup_inputs():
    n = np.random.standard_normal
    s = mx_kscale(K)[:, None]
    s2 = mx_kscale(K2)[:, None]
    u = mx_kscale(H)[:, None]
    tab_words, tab_scales = pack_weight(n((K, T)) * s, "e4m3")
    tab2_words, tab2_scales = pack_weight(n((K2, T)) * s2, "e4m3")
    w4_words, w4_scales = pack_weight(n((K2, H)) / np.sqrt(K2) / s2 * u.T, "e2m1")
    w8_words, w8_scales = pack_weight(n((K2, H)) / np.sqrt(K2) / s2 * u.T, "e4m3")
    perm = np.random.permutation(T2)
    return {
        "tab_words": tab_words, "tab_scales": tab_scales,
        "tab2_words": tab2_words, "tab2_scales": tab2_scales,
        "offs": striped(np.random.permutation(T)[:S]),
        "offs2": striped(np.random.permutation(T)[:S]),
        "offs3": striped(perm[:S]), "offs4": striped(perm[S:]),
        "w1": (n((K, H)) / np.sqrt(K) / s * u.T).astype(np.float32),
        "w4_words": w4_words, "w4_scales": w4_scales,
        "w8_words": w8_words, "w8_scales": w8_scales,
        "al": np.random.uniform(0.2, 0.8, H).astype(np.float32),
        "wg1": np.exp(0.3 * n((128, S))).astype(np.float32),
        "wg2": np.exp(0.3 * n((128, S))).astype(np.float32),
        "lo": (-np.random.uniform(0.6, 1.6, H) * u[:, 0]).astype(np.float32),
        "hi": (np.random.uniform(0.6, 1.6, H) * u[:, 0]).astype(np.float32),
        "wd": (n((H, N)) / np.sqrt(H) / u).astype(np.float32),
    }

def reference(tab_words, tab_scales, tab2_words, tab2_scales, offs, offs2, offs3, offs4, w1, w4_words, w4_scales, w8_words, w8_scales, al, wg1, wg2, lo, hi, wd):
    v = unpack_weight(tab_words, tab_scales, "e4m3")[:, unstriped(offs)]
    v2 = unpack_weight(tab2_words, tab2_scales, "e4m3")[:, unstriped(offs2)]
    h1 = mxq(f64(w1), 0, "e4m3").T @ v
    fw = unpack_weight(w4_words, w4_scales, "e2m1").T @ v2
    bw = unpack_weight(w8_words, w8_scales, "e4m3").T @ v2
    h2 = fw + f64(al)[:, None] * (bw - fw)
    page = np.zeros((H, T2))
    page[:, unstriped(offs3)] = np.tile(f64(wg1), (H // 128, 1)) * h1
    page[:, unstriped(offs4)] = np.tile(f64(wg2), (H // 128, 1)) * h2
    z = np.minimum(np.maximum(page, f64(lo)[:, None]), f64(hi)[:, None])
    return mxq(f64(wd), 0, "e4m3").T @ mxq(z, 0, "e4m3")

@@ -1,0 +1,342 @@
+from contextlib import ExitStack
+
+import concourse.mybir as mybir
+from concourse.masks import make_identity
+
+F32 = mybir.dt.float32
+BF16 = mybir.dt.bfloat16
+I32 = mybir.dt.int32
+U32 = mybir.dt.uint32
+U16 = mybir.dt.uint16
+U8 = mybir.dt.uint8
+FP8X4 = mybir.dt.float8_e4m3fn_x4
+FP4X4 = mybir.dt.float4_e2m1fn_x4
+ALU = mybir.AluOpType
+COPY = mybir.ActivationFunctionType.Copy
+
+K, K2, H, N, T, S, T2 = 1024, 512, 1024, 256, 2048, 1024, 2048
+FLOPS = 2 * (K * H * S + 2 * K2 * H * S + H * N * T2)
+
+P = 128
+PACK = 4
+PASS = P * PACK
+BANK = 512
+QUADS = 4
+QUAD = 32
+SLICES = H // P
+
+
+def tile_list_woven_post_filter_kernel(
+    tc, tab_words, tab_scales, tab2_words, tab2_scales, offs, offs2, offs3, offs4,
+    w1, w4_words, w4_scales, w8_words, w8_scales, al, wg1, wg2, lo, hi, wd, out,
+):
+    nc = tc.nc
+    with ExitStack() as ctx:
+        lists = ctx.enter_context(tc.tile_pool(name="lists", bufs=1))
+        held = ctx.enter_context(tc.tile_pool(name="held", bufs=1))
+        tables = ctx.enter_context(tc.tile_pool(name="tables", bufs=1))
+        ring = ctx.enter_context(tc.tile_pool(name="ring", bufs=2))
+        psum = ctx.enter_context(tc.psum_pool(name="psum", bufs=1))
+
+        banks = [psum.tile([P, BANK], F32, name="bank%d" % i) for i in range(8)]
+
+        def load_list(source, name):
+            tile = lists.tile([P, S // 16], U16, name=name)
+            nc.sync.dma_start(tile[:], source)
+            return tile
+
+        def load_words(pool, source, columns, name, **where):
+            tile = pool.tile([P, columns], I32, name=name, align_bytes=64, **where)
+            nc.sync.dma_start(tile[:], source.bitcast(I32))
+            return tile
+
+        def zeroed_plane(pool, columns, name, **where):
+            tile = pool.tile([P, columns], U8, name=name, align_bytes=64, **where)
+            nc.vector.memset(tile[:].bitcast(I32), 0)
+            return tile
+
+        def load_scale_rows(plane, first_row, source):
+            for q in range(QUADS):
+                row = QUAD * q + first_row
+                nc.scalar.dma_start(plane[row : row + 4, :].bitcast(I32), source[4 * q : 4 * q + 4, :].bitcast(I32))
+
+        def load_channel_vector(source, name):
+            tile = held.tile([P, 2, PACK], F32, name=name)
+            nc.sync.dma_start(tile[:], source.rearrange("(b p t) -> p b t", p=P, t=PACK))
+            return tile
+
+        def load_gains(source, t, name):
+            tile = held.tile([P, S], F32, name=name)
+            rows = source.rearrange("(q t) j -> q t j", t=PACK)
+            for q in range(QUADS):
+                nc.sync.dma_start(tile[QUAD * q : QUAD * (q + 1), :], rows[:, t, :])
+            return tile
+
+        def gather(dtype, table, offsets, name):
+            tile = held.tile([P, S], dtype, name=name, align_bytes=64)
+            nc.vector.tensor_copy(tile[:], table[:].bitcast(dtype).indirect(offsets[:]))
+            return tile
+
+        word_bytes = 4 * T
+        tab2_plane = zeroed_plane(tables, T, "tab2_plane", offset=3 * word_bytes)
+        w48_plane = zeroed_plane(held, H, "w48_plane")
+        tab_plane = zeroed_plane(tables, T, "tab_plane", offset=3 * word_bytes + T)
+
+        list2 = load_list(offs2, "list2")
+        tab2_w = load_words(tables, tab2_words[0].rearrange("p t i -> p (t i)"), T, "tab2_w", offset=0)
+        load_scale_rows(tab2_plane, 0, tab2_scales[0])
+        w4_raw = load_words(ring, w4_words[0], H // 2, "w4_raw", tag="turned")
+        w8_raw = load_words(ring, w8_words[0].rearrange("p c i -> p (c i)"), H, "w8_raw", tag="h1")
+        load_scale_rows(w48_plane, 0, w4_scales[0])
+        load_scale_rows(w48_plane, 4, w8_scales[0])
+        al_t = load_channel_vector(al, "al_t")
+        list1 = load_list(offs, "list1")
+        tab_w = [
+            load_words(tables, tab_words[a].rearrange("p t i -> p (t i)"), T, "tab_w%d" % a, offset=(1 + a) * word_bytes)
+            for a in range(2)
+        ]
+        for a in range(2):
+            load_scale_rows(tab_plane, 4 * a, tab_scales[a])
+        list4 = load_list(offs4, "list4")
+        list3 = load_list(offs3, "list3")
+
+        def load_w1(b):
+            raw = ring.tile([P, 2 * PACK * PASS], F32, name="w1_raw", tag="wide", align_bytes=64)
+            views = []
+            for a in range(2):
+                view = raw[:, a * PACK * PASS : (a + 1) * PACK * PASS].rearrange("p (j c) -> p j c", j=PACK)
+                rows = w1[PASS * a : PASS * (a + 1), PASS * b : PASS * (b + 1)]
+                nc.sync.dma_start(view, rows.rearrange("(p j) c -> p j c", j=PACK))
+                views.append(view)
+            return views
+
+        gain2 = [load_gains(wg2, 0, "gain2_0")]
+        w1_raw = [load_w1(0)]
+        gain2.append(load_gains(wg2, 1, "gain2_1"))
+        gain2.append(load_gains(wg2, 2, "gain2_2"))
+        gain1 = [load_gains(wg1, 0, "gain1_0")]
+        lo_t = load_channel_vector(lo, "lo_t")
+        hi_t = load_channel_vector(hi, "hi_t")
+        gain1.append(load_gains(wg1, 1, "gain1_1"))
+        gain1.append(load_gains(wg1, 2, "gain1_2"))
+        gain2.append(load_gains(wg2, 3, "gain2_3"))
+        gain1.append(load_gains(wg1, 3, "gain1_3"))
+        w1_raw.append(load_w1(1))
+        wd_raw = ring.tile([P, 2, PACK, N], F32, name="wd_raw", tag="result")
+        for b in range(2):
+            nc.sync.dma_start(wd_raw[:, b, :, :], wd[PASS * b : PASS * (b + 1), :].rearrange("(p j) n -> p j n", j=PACK))
+
+        ident = held.tile([P, P], F32, name="ident")
+        make_identity(nc, ident[:])
+
+        rest_t = held.tile([P, 2, PACK], F32, name="rest_t")
+        nc.vector.tensor_scalar(rest_t[:], al_t[:], -1.0, 1.0, ALU.mult, ALU.add)
+
+        v2_words = gather(U32, tab2_w, list2, "v2_words")
+        v2_plane = gather(U8, tab2_plane, list2, "v2_plane")
+
+        def reorder_columns(dtype, source, name, columns):
+            tile = held.tile([P, columns], source.dtype, name=name, align_bytes=64)
+            nc.vector.tensor_copy(
+                tile[:].bitcast(dtype).rearrange("p (b t c i) -> p b c t i", b=2, t=PACK, i=4),
+                source[:].bitcast(dtype).rearrange("p (b c i t) -> p b c t i", b=2, t=PACK, i=4),
+            )
+            return tile
+
+        w4 = reorder_columns(U16, w4_raw, "w4", H // 2)
+        w8 = reorder_columns(U32, w8_raw, "w8", H)
+        w48_scales = reorder_columns(U8, w48_plane, "w48_scales", H)
+
+        v_words = [gather(U32, tab_w[a], list1, "v_words%d" % a) for a in range(2)]
+        v_plane = gather(U8, tab_plane, list1, "v_plane")
+
+        def blend(s, last_turned=None):
+            b, t = divmod(s, PACK)
+            h2 = ring.tile([P, S], F32, name="h2", bufs=3)
+            cols = slice(P * s, P * (s + 1))
+            for half in range(S // BANK):
+                j = slice(BANK * half, BANK * (half + 1))
+                fw, bw = banks[2 * half], banks[2 * half + 1]
+                turn, back = banks[4 + 2 * half], banks[5 + 2 * half]
+                moving = v2_words[:, j].bitcast(FP8X4)
+                nc.tensor.matmul_mx(
+                    fw[:], lhsT=w4[:].bitcast(U8)[:, 2 * P * s : 2 * P * (s + 1)].bitcast(FP4X4), lhsT_scale=w48_scales[:, cols],
+                    rhs=moving, rhs_scale=v2_plane[:, j], start=True, stop=True,
+                )
+                nc.tensor.matmul_mx(
+                    bw[:], lhsT=w8[:, cols].bitcast(FP8X4), lhsT_scale=w48_scales[4:P, cols],
+                    rhs=moving, rhs_scale=v2_plane[:, j], start=True, stop=True,
+                )
+                fw_part = ring.tile([P, BANK], F32, name="fw_part")
+                bw_part = ring.tile([P, BANK], F32, name="bw_part")
+                nc.scalar.activation(fw_part[:], fw[:], COPY, scale=rest_t[:, b, t : t + 1])
+                nc.scalar.activation(bw_part[:], bw[:], COPY, scale=al_t[:, b, t : t + 1])
+                for block in range(BANK // P):
+                    c = slice(P * block, P * (block + 1))
+                    nc.tensor.matmul(turn[:, c], fw_part[:, c], ident[:], is_transpose=True, start=True, stop=False)
+                    nc.tensor.matmul(turn[:, c], bw_part[:, c], ident[:], is_transpose=True, start=False, stop=True)
+                if last_turned is not None and half == 1:
+                    turned = last_turned
+                else:
+                    turned = ring.tile([P, BANK], F32, name="turned", tag="turned", align_bytes=64)[:]
+                nc.scalar.copy(turned, turn[:])
+                for block in range(BANK // P):
+                    c = slice(P * block, P * (block + 1))
+                    nc.tensor.transpose(back[:, c], turned[:, c], ident[:])
+                nc.scalar.copy(h2[:, j], back[:])
+            return h2
+
+        def quantise_w1(b, **where):
+            grouped = ring.tile([P, 2 * PASS * PACK], BF16, name="w1_grouped", align_bytes=64, **where)
+            for a in range(2):
+                nc.scalar.copy(
+                    grouped[:, a * PASS * PACK : (a + 1) * PASS * PACK].rearrange("p (t m j) -> p m t j", t=PACK, j=PACK),
+                    w1_raw[b][a].rearrange("p j (m t) -> p m t j", t=PACK),
+                )
+            codes = held.tile([P, 2 * PASS], U32, name="w1_codes%d" % b, align_bytes=64)
+            plane = held.tile([P, 2 * PASS], U8, name="w1_plane%d" % b, align_bytes=64)
+            nc.vector.quantize_mx(codes[:].bitcast(FP8X4), plane[:], grouped[:])
+            return codes, plane
+
+        def features(s, w1_mx):
+            b, t = divmod(s, PACK)
+            codes, plane = w1_mx
+            h1 = ring.tile([P, S], F32, name="h1", tag="h1", align_bytes=64)
+            for half in range(S // BANK):
+                j = slice(BANK * half, BANK * (half + 1))
+                bank = banks[7]
+                for a in range(2):
+                    cols = slice(PASS * a + P * t, PASS * a + P * (t + 1))
+                    nc.tensor.matmul_mx(
+                        bank[:], lhsT=codes[:, cols].bitcast(FP8X4), lhsT_scale=plane[:, cols],
+                        rhs=v_words[a][:, j].bitcast(FP8X4), rhs_scale=v_plane[4 * a : P, j],
+                        start=(a == 0), stop=(a == 1),
+                    )
+                nc.scalar.copy(h1[:, j], bank[:])
+            return h1
+
+        def new_page():
+            return ring.tile([P, T2], F32, name="page", tag="page", bufs=3, align_bytes=64)
+
+        def put(page, offsets, values, gains):
+            nc.vector.tensor_tensor(page[:].indirect(offsets[:]), values[:], gains[:], ALU.mult)
+
+        clamped = [
+            tables.tile([P, PACK, T2], BF16, name="clamped%d" % b, offset=2 * PACK * T2 * b, align_bytes=64) for b in range(2)
+        ]
+        nc.gpsimd.memset(clamped[1][:, PACK - 1, :], 0.0)
+
+        def clamp(target, page_part, s):
+            b, t = divmod(s, PACK)
+            nc.vector.tensor_scalar(target, page_part, lo_t[:, b, t : t + 1], hi_t[:, b, t : t + 1], ALU.max, ALU.min)
+
+        def clamp_page(page, s):
+            b, t = divmod(s, PACK)
+            clamp(clamped[b][:, t, :], page[:], s)
+
+        def weave(b, half):
+            c0 = half * T2 // 2
+            nc.scalar.copy(
+                woven[b][:, PACK * c0 : PACK * (c0 + T2 // 2)].rearrange("p (c i t) -> p c t i", t=PACK, i=4),
+                clamped[b][:, :, c0 : c0 + T2 // 2].rearrange("p t (c i) -> p c t i", i=4),
+            )
+
+        def new_woven(b):
+            woven[b] = ring.tile([P, PACK * T2], BF16, name="woven", tag="wide", align_bytes=64)
+            middle = PACK * T2 // 2
+            return woven[b][:, middle - BANK : middle + BANK].bitcast(F32)
+
+        pages = {}
+        z_codes = [None, None]
+        z_plane = [held.tile([P, T2], U8, name="z_plane%d" % b, align_bytes=64) for b in range(2)]
+        woven = {}
+
+        def quantise_z(b, source, c0, width):
+            nc.vector.quantize_mx(z_codes[b][:, c0 : c0 + width].bitcast(FP8X4), z_plane[b][:, c0 : c0 + width], source)
+
+        def put_second(s, last_turned=None):
+            values = blend(s, last_turned)
+            if s not in pages:
+                pages[s] = new_page()
+            put(pages[s], list4, values, gain2[s % PACK])
+
+        def put_first(s):
+            put(pages[s], list3, features(s, w1_mx[s // PACK]), gain1[s % PACK])
+
+        put_second(0)
+        put_second(1)
+        w1_mx = [quantise_w1(0, tag="page", bufs=3)]
+        put_second(2)
+        put_first(0)
+        put_first(1)
+        clamp_page(pages[0], 0)
+        put_second(3)
+        clamp_page(pages[1], 1)
+        put_first(2)
+        w1_mx.append(quantise_w1(1, tag="codes"))
+        put_first(3)
+        clamp_page(pages[2], 2)
+        put_second(4)
+        clamp_page(pages[3], 3)
+        wd_grouped = held.tile([P, 2, N, PACK], BF16, name="wd_grouped", align_bytes=64)
+        nc.scalar.copy(wd_grouped[:], wd_raw[:].rearrange("p b j n -> p b n j"))
+        wd_codes = held.tile([P, 2 * N], U32, name="wd_codes", align_bytes=64)
+        wd_plane = held.tile([P, 2 * N], U8, name="wd_plane", align_bytes=64)
+        nc.vector.quantize_mx(wd_codes[:].bitcast(FP8X4), wd_plane[:], wd_grouped[:].rearrange("p b n j -> p (b n j)"))
+        put_first(4)
+        put_second(5, new_woven(0))
+        clamp_page(pages[4], 4)
+        weave(0, 0)
+        z_codes[0] = ring.tile([P, T2], U32, name="z_codes0", tag="codes", align_bytes=64)
+        quantise_z(0, woven[0][:, : PACK * T2 // 2], 0, T2 // 2)
+        put_first(5)
+        put_second(6)
+        clamp_page(pages[5], 5)
+        weave(0, 1)
+        quantise_z(0, woven[0][:, PACK * T2 // 2 :], T2 // 2, T2 // 2)
+        put_first(6)
+        clamp_page(pages[6], 6)
+        pages[7] = new_page()
+        put_first(7)
+        put_second(7, new_woven(1))
+        for half in range(2):
+            weave(1, half)
+
+        z_codes[1] = ring.tile([P, T2], U32, name="z_codes1", tag="codes", align_bytes=64)
+        results = [ring.tile([P, T2], F32, name="result%d" % n, tag="result") for n in range(N // P)]
+
+        def filter_pass(b, chunk):
+            cols = slice(BANK * chunk, BANK * (chunk + 1))
+            for n in range(N // P):
+                w_cols = slice(N * b + P * n, N * b + P * (n + 1))
+                nc.tensor.matmul_mx(
+                    banks[2 * chunk + n][:], lhsT=wd_codes[:, w_cols].bitcast(FP8X4), lhsT_scale=wd_plane[:, w_cols],
+                    rhs=z_codes[b][:, cols].bitcast(FP8X4), rhs_scale=z_plane[b][:, cols],
+                    start=(b == 0), stop=(b == 1),
+                )
+
+        for chunk in range(T2 // BANK):
+            filter_pass(0, chunk)
+        last = SLICES - 1
+        chunks = T2 // BANK
+
+        def piece(chunk):
+            return woven[1][:, chunk * PACK * BANK : (chunk + 1) * PACK * BANK]
+
+        def clamp_last(chunk):
+            target = piece(chunk).rearrange("p (c t) -> p c t", t=PACK)[:, :, PACK - 1]
+            clamp(target, pages[last][:, BANK * chunk : BANK * (chunk + 1)], last)
+
+        clamp_last(0)
+        for chunk in range(chunks):
+            cols = slice(BANK * chunk, BANK * (chunk + 1))
+            if chunk + 1 < chunks:
+                clamp_last(chunk + 1)
+            quantise_z(1, piece(chunk), BANK * chunk, BANK)
+            filter_pass(1, chunk)
+            for n in range(N // P):
+                if chunk == chunks - 1 and n == 1:
+                    nc.vector.tensor_copy(results[n][:, cols], banks[2 * chunk + n][:])
+                else:
+                    nc.scalar.copy(results[n][:, cols], banks[2 * chunk + n][:])
+                nc.sync.dma_start(out[P * n : P * (n + 1), cols], results[n][:, cols])

@@ -24,6 +24,9 @@ BANK = 512
 QUADS = 4
 QUAD = 32
 SLICES = H // P
+H_BUFS = 2
+PAGES = 4
+PART_BUFS = 4
 
 
 def tile_list_woven_post_filter_kernel(
@@ -86,7 +89,7 @@ def tile_list_woven_post_filter_kernel(
         tab2_w = load_words(tables, tab2_words[0].rearrange("p t i -> p (t i)"), T, "tab2_w", offset=0)
         load_scale_rows(tab2_plane, 0, tab2_scales[0])
         w4_raw = load_words(ring, w4_words[0], H // 2, "w4_raw", tag="turned")
-        w8_raw = load_words(ring, w8_words[0].rearrange("p c i -> p (c i)"), H, "w8_raw", tag="h1")
+        w8_raw = load_words(ring, w8_words[0].rearrange("p c i -> p (c i)"), H, "w8_raw", tag="h", bufs=H_BUFS)
         load_scale_rows(w48_plane, 0, w4_scales[0])
         load_scale_rows(w48_plane, 4, w8_scales[0])
         al_t = load_channel_vector(al, "al_t")
@@ -95,8 +98,10 @@ def tile_list_woven_post_filter_kernel(
             load_words(tables, tab_words[a].rearrange("p t i -> p (t i)"), T, "tab_w%d" % a, offset=(1 + a) * word_bytes)
             for a in range(2)
         ]
-        for a in range(2):
-            load_scale_rows(tab_plane, 4 * a, tab_scales[a])
+        for q in range(QUADS):
+            nc.scalar.dma_start(
+                tab_plane[QUAD * q : QUAD * q + 8, :].bitcast(I32), tab_scales[:, 4 * q : 4 * q + 4, :].bitcast(I32)
+            )
         list4 = load_list(offs4, "list4")
         list3 = load_list(offs3, "list3")
 
@@ -112,17 +117,16 @@ def tile_list_woven_post_filter_kernel(
 
         gain2 = [load_gains(wg2, 0, "gain2_0")]
         w1_raw = [load_w1(0)]
-        gain2.append(load_gains(wg2, 1, "gain2_1"))
-        gain2.append(load_gains(wg2, 2, "gain2_2"))
+        for t in range(1, PACK):
+            gain2.append(load_gains(wg2, t, "gain2_%d" % t))
         gain1 = [load_gains(wg1, 0, "gain1_0")]
         lo_t = load_channel_vector(lo, "lo_t")
         hi_t = load_channel_vector(hi, "hi_t")
         gain1.append(load_gains(wg1, 1, "gain1_1"))
         gain1.append(load_gains(wg1, 2, "gain1_2"))
-        gain2.append(load_gains(wg2, 3, "gain2_3"))
-        gain1.append(load_gains(wg1, 3, "gain1_3"))
         w1_raw.append(load_w1(1))
-        wd_raw = ring.tile([P, 2, PACK, N], F32, name="wd_raw", tag="result")
+        gain1.append(load_gains(wg1, 3, "gain1_3"))
+        wd_raw = ring.tile([P, 2, PACK, N], F32, name="wd_raw", tag="codes", align_bytes=64)
         for b in range(2):
             nc.sync.dma_start(wd_raw[:, b, :, :], wd[PASS * b : PASS * (b + 1), :].rearrange("(p j) n -> p j n", j=PACK))
 
@@ -150,9 +154,8 @@ def tile_list_woven_post_filter_kernel(
         v_words = [gather(U32, tab_w[a], list1, "v_words%d" % a) for a in range(2)]
         v_plane = gather(U8, tab_plane, list1, "v_plane")
 
-        def blend(s, last_turned=None):
+        def blend(s, h2, staging):
             b, t = divmod(s, PACK)
-            h2 = ring.tile([P, S], F32, name="h2", bufs=3)
             cols = slice(P * s, P * (s + 1))
             for half in range(S // BANK):
                 j = slice(BANK * half, BANK * (half + 1))
@@ -167,16 +170,16 @@ def tile_list_woven_post_filter_kernel(
                     bw[:], lhsT=w8[:, cols].bitcast(FP8X4), lhsT_scale=w48_scales[4:P, cols],
                     rhs=moving, rhs_scale=v2_plane[:, j], start=True, stop=True,
                 )
-                fw_part = ring.tile([P, BANK], F32, name="fw_part")
-                bw_part = ring.tile([P, BANK], F32, name="bw_part")
+                fw_part = ring.tile([P, BANK], F32, name="fw_part", tag="fw_part", bufs=PART_BUFS)
+                bw_part = ring.tile([P, BANK], F32, name="bw_part", tag="bw_part", bufs=PART_BUFS)
                 nc.scalar.activation(fw_part[:], fw[:], COPY, scale=rest_t[:, b, t : t + 1])
                 nc.scalar.activation(bw_part[:], bw[:], COPY, scale=al_t[:, b, t : t + 1])
                 for block in range(BANK // P):
                     c = slice(P * block, P * (block + 1))
                     nc.tensor.matmul(turn[:, c], fw_part[:, c], ident[:], is_transpose=True, start=True, stop=False)
                     nc.tensor.matmul(turn[:, c], bw_part[:, c], ident[:], is_transpose=True, start=False, stop=True)
-                if last_turned is not None and half == 1:
-                    turned = last_turned
+                if half in staging:
+                    turned = staging[half]
                 else:
                     turned = ring.tile([P, BANK], F32, name="turned", tag="turned", align_bytes=64)[:]
                 nc.scalar.copy(turned, turn[:])
@@ -184,10 +187,8 @@ def tile_list_woven_post_filter_kernel(
                     c = slice(P * block, P * (block + 1))
                     nc.tensor.transpose(back[:, c], turned[:, c], ident[:])
                 nc.scalar.copy(h2[:, j], back[:])
-            return h2
 
-        def quantise_w1(b, **where):
-            grouped = ring.tile([P, 2 * PASS * PACK], BF16, name="w1_grouped", align_bytes=64, **where)
+        def quantise_w1(b, grouped):
             for a in range(2):
                 nc.scalar.copy(
                     grouped[:, a * PASS * PACK : (a + 1) * PASS * PACK].rearrange("p (t m j) -> p m t j", t=PACK, j=PACK),
@@ -198,10 +199,9 @@ def tile_list_woven_post_filter_kernel(
             nc.vector.quantize_mx(codes[:].bitcast(FP8X4), plane[:], grouped[:])
             return codes, plane
 
-        def features(s, w1_mx):
+        def features(s, h1):
             b, t = divmod(s, PACK)
-            codes, plane = w1_mx
-            h1 = ring.tile([P, S], F32, name="h1", tag="h1", align_bytes=64)
+            codes, plane = w1_mx[b]
             for half in range(S // BANK):
                 j = slice(BANK * half, BANK * (half + 1))
                 bank = banks[7]
@@ -213,97 +213,108 @@ def tile_list_woven_post_filter_kernel(
                         start=(a == 0), stop=(a == 1),
                     )
                 nc.scalar.copy(h1[:, j], bank[:])
-            return h1
 
-        def new_page():
-            return ring.tile([P, T2], F32, name="page", tag="page", bufs=3, align_bytes=64)
+        pages = {}
 
-        def put(page, offsets, values, gains):
-            nc.vector.tensor_tensor(page[:].indirect(offsets[:]), values[:], gains[:], ALU.mult)
+        def put(s, offsets, values, gains):
+            if s not in pages:
+                pages[s] = ring.tile([P, T2], F32, name="page", tag="page", bufs=PAGES, align_bytes=64)
+            weighted = ring.tile([P, S], F32, name="weighted", tag="weighted", bufs=3)
+            nc.gpsimd.tensor_tensor(weighted[:], values, gains[:], ALU.mult)
+            nc.vector.tensor_copy(pages[s][:].indirect(offsets[:]), weighted[:])
 
         clamped = [
-            tables.tile([P, PACK, T2], BF16, name="clamped%d" % b, offset=2 * PACK * T2 * b, align_bytes=64) for b in range(2)
+            tables.tile([P, PACK * T2], BF16, name="clamped%d" % b, offset=2 * PACK * T2 * b, align_bytes=64) for b in range(2)
         ]
-        nc.gpsimd.memset(clamped[1][:, PACK - 1, :], 0.0)
 
-        def clamp(target, page_part, s):
+        def clamped_row(s):
             b, t = divmod(s, PACK)
-            nc.vector.tensor_scalar(target, page_part, lo_t[:, b, t : t + 1], hi_t[:, b, t : t + 1], ALU.max, ALU.min)
+            return clamped[b][:, T2 * t : T2 * (t + 1)]
 
-        def clamp_page(page, s):
+        nc.gpsimd.memset(clamped_row(SLICES - 1), 0.0)
+
+        def clamp(engine, target, page_part, s):
             b, t = divmod(s, PACK)
-            clamp(clamped[b][:, t, :], page[:], s)
+            engine.tensor_scalar(target, page_part, hi_t[:, b, t : t + 1], lo_t[:, b, t : t + 1], ALU.min, ALU.max)
+
+        def clamp_page(s):
+            clamp(nc.gpsimd, clamped_row(s), pages[s][:], s)
 
         def weave(b, half):
             c0 = half * T2 // 2
             nc.scalar.copy(
                 woven[b][:, PACK * c0 : PACK * (c0 + T2 // 2)].rearrange("p (c i t) -> p c t i", t=PACK, i=4),
-                clamped[b][:, :, c0 : c0 + T2 // 2].rearrange("p t (c i) -> p c t i", i=4),
+                clamped[b][:].rearrange("p (t c) -> p t c", t=PACK)[:, :, c0 : c0 + T2 // 2].rearrange("p t (c i) -> p c t i", i=4),
             )
 
-        def new_woven(b):
-            woven[b] = ring.tile([P, PACK * T2], BF16, name="woven", tag="wide", align_bytes=64)
-            middle = PACK * T2 // 2
-            return woven[b][:, middle - BANK : middle + BANK].bitcast(F32)
+        def bank_view(tile, first):
+            return tile[:, first : first + 2 * BANK].bitcast(F32)
 
-        pages = {}
         z_codes = [None, None]
         z_plane = [held.tile([P, T2], U8, name="z_plane%d" % b, align_bytes=64) for b in range(2)]
-        woven = {}
 
         def quantise_z(b, source, c0, width):
             nc.vector.quantize_mx(z_codes[b][:, c0 : c0 + width].bitcast(FP8X4), z_plane[b][:, c0 : c0 + width], source)
 
-        def put_second(s, last_turned=None):
-            values = blend(s, last_turned)
-            if s not in pages:
-                pages[s] = new_page()
-            put(pages[s], list4, values, gain2[s % PACK])
+        def values_tile(before_clamp):
+            if before_clamp is not None:
+                return clamped_row(before_clamp).bitcast(F32)
+            return ring.tile([P, S], F32, name="h", tag="h", bufs=H_BUFS, align_bytes=64)[:]
 
-        def put_first(s):
-            put(pages[s], list3, features(s, w1_mx[s // PACK]), gain1[s % PACK])
+        def put_second(s, staging, before_clamp=None):
+            values = values_tile(before_clamp)
+            blend(s, values, staging)
+            put(s, list4, values, gain2[s % PACK])
 
-        put_second(0)
-        put_second(1)
-        w1_mx = [quantise_w1(0, tag="page", bufs=3)]
-        put_second(2)
+        def put_first(s, before_clamp=None):
+            values = values_tile(before_clamp)
+            features(s, values)
+            put(s, list3, values, gain1[s % PACK])
+
+        for s in range(PAGES - 1):
+            put_second(s, {})
+        w1_grouped = ring.tile([P, 2 * PASS * PACK], BF16, name="w1_grouped0", tag="page", bufs=PAGES, align_bytes=64)
+        w1_mx = [quantise_w1(0, w1_grouped)]
+        put_second(3, {})
         put_first(0)
-        put_first(1)
-        clamp_page(pages[0], 0)
-        put_second(3)
-        clamp_page(pages[1], 1)
-        put_first(2)
-        w1_mx.append(quantise_w1(1, tag="codes"))
+        put_first(1, 0)
+        clamp_page(0)
+        put_first(2, 1)
+        clamp_page(1)
+        w1_grouped = ring.tile([P, 2 * PASS * PACK], BF16, name="w1_grouped1", tag="codes", align_bytes=64)
+        put_second(4, {1: bank_view(w1_grouped, PASS * PACK - BANK)}, 2)
+        clamp_page(2)
         put_first(3)
-        clamp_page(pages[2], 2)
-        put_second(4)
-        clamp_page(pages[3], 3)
-        wd_grouped = held.tile([P, 2, N, PACK], BF16, name="wd_grouped", align_bytes=64)
-        nc.scalar.copy(wd_grouped[:], wd_raw[:].rearrange("p b j n -> p b n j"))
+        w1_mx.append(quantise_w1(1, w1_grouped))
+        wd_grouped = held.tile([P, 2 * N * PACK], BF16, name="wd_grouped", align_bytes=64)
+        put_second(5, {1: bank_view(wd_grouped, 0)}, 3)
+        clamp_page(3)
+        put_first(4)
+        nc.scalar.copy(
+            wd_grouped[:].rearrange("p (b n j) -> p b n j", b=2, j=PACK), wd_raw[:].rearrange("p b j n -> p b n j")
+        )
         wd_codes = held.tile([P, 2 * N], U32, name="wd_codes", align_bytes=64)
         wd_plane = held.tile([P, 2 * N], U8, name="wd_plane", align_bytes=64)
-        nc.vector.quantize_mx(wd_codes[:].bitcast(FP8X4), wd_plane[:], wd_grouped[:].rearrange("p b n j -> p (b n j)"))
-        put_first(4)
-        put_second(5, new_woven(0))
-        clamp_page(pages[4], 4)
+        nc.vector.quantize_mx(wd_codes[:].bitcast(FP8X4), wd_plane[:], wd_grouped[:])
+        middle = PACK * T2 // 2
+        woven = [ring.tile([P, PACK * T2], BF16, name="woven%d" % b, tag="wide", align_bytes=64) for b in range(2)]
+        put_second(6, {1: bank_view(woven[0], 0)}, 4)
+        clamp_page(4)
+        put_first(5)
         weave(0, 0)
         z_codes[0] = ring.tile([P, T2], U32, name="z_codes0", tag="codes", align_bytes=64)
-        quantise_z(0, woven[0][:, : PACK * T2 // 2], 0, T2 // 2)
-        put_first(5)
-        put_second(6)
-        clamp_page(pages[5], 5)
+        quantise_z(0, woven[0][:, :middle], 0, T2 // 2)
+        put_first(6, 5)
+        clamp_page(5)
+        put_first(7, 6)
+        clamp_page(6)
+        put_second(7, {0: bank_view(woven[0], middle), 1: bank_view(woven[1], middle - BANK)})
         weave(0, 1)
-        quantise_z(0, woven[0][:, PACK * T2 // 2 :], T2 // 2, T2 // 2)
-        put_first(6)
-        clamp_page(pages[6], 6)
-        pages[7] = new_page()
-        put_first(7)
-        put_second(7, new_woven(1))
+        quantise_z(0, woven[0][:, middle:], T2 // 2, T2 // 2)
         for half in range(2):
             weave(1, half)
 
         z_codes[1] = ring.tile([P, T2], U32, name="z_codes1", tag="codes", align_bytes=64)
-        results = [ring.tile([P, T2], F32, name="result%d" % n, tag="result") for n in range(N // P)]
 
         def filter_pass(b, chunk):
             cols = slice(BANK * chunk, BANK * (chunk + 1))
@@ -325,7 +336,7 @@ def tile_list_woven_post_filter_kernel(
 
         def clamp_last(chunk):
             target = piece(chunk).rearrange("p (c t) -> p c t", t=PACK)[:, :, PACK - 1]
-            clamp(target, pages[last][:, BANK * chunk : BANK * (chunk + 1)], last)
+            clamp(nc.vector, target, pages[last][:, BANK * chunk : BANK * (chunk + 1)], last)
 
         clamp_last(0)
         for chunk in range(chunks):
@@ -335,8 +346,9 @@ def tile_list_woven_post_filter_kernel(
             quantise_z(1, piece(chunk), BANK * chunk, BANK)
             filter_pass(1, chunk)
             for n in range(N // P):
+                result = ring.tile([P, BANK], F32, name="result", tag=("fw_part", "bw_part")[n], bufs=PART_BUFS)
                 if chunk == chunks - 1 and n == 1:
-                    nc.vector.tensor_copy(results[n][:, cols], banks[2 * chunk + n][:])
+                    nc.vector.tensor_copy(result[:], banks[2 * chunk + n][:])
                 else:
-                    nc.scalar.copy(results[n][:, cols], banks[2 * chunk + n][:])
-                nc.sync.dma_start(out[P * n : P * (n + 1), cols], results[n][:, cols])
+                    nc.scalar.copy(result[:], banks[2 * chunk + n][:])
+                nc.sync.dma_start(out[P * n : P * (n + 1), cols], result[:])

@@ -1,7 +1,6 @@
 from contextlib import ExitStack
 
 import concourse.mybir as mybir
-from concourse.masks import make_identity
 
 F32 = mybir.dt.float32
 BF16 = mybir.dt.bfloat16
@@ -53,15 +52,15 @@ def tile_list_woven_post_filter_kernel(
             nc.sync.dma_start(tile[:], source.bitcast(I32))
             return tile
 
-        def zeroed_plane(pool, columns, name, **where):
+        def zeroed_plane(engine, pool, columns, name, **where):
             tile = pool.tile([P, columns], U8, name=name, align_bytes=64, **where)
-            nc.vector.memset(tile[:].bitcast(I32), 0)
+            engine.memset(tile[:].bitcast(I32), 0)
             return tile
 
         def load_scale_rows(plane, first_row, source):
             for q in range(QUADS):
                 row = QUAD * q + first_row
-                nc.scalar.dma_start(plane[row : row + 4, :].bitcast(I32), source[4 * q : 4 * q + 4, :].bitcast(I32))
+                nc.sync.dma_start(plane[row : row + 4, :].bitcast(I32), source[4 * q : 4 * q + 4, :].bitcast(I32))
 
         def load_channel_vector(source, name):
             tile = held.tile([P, 2, PACK], F32, name=name)
@@ -81,29 +80,28 @@ def tile_list_woven_post_filter_kernel(
             return tile
 
         word_bytes = 4 * T
-        tab2_plane = zeroed_plane(tables, T, "tab2_plane", offset=3 * word_bytes)
-        w48_plane = zeroed_plane(held, H, "w48_plane")
-        tab_plane = zeroed_plane(tables, T, "tab_plane", offset=3 * word_bytes + T)
+        tab2_plane = zeroed_plane(nc.gpsimd, tables, T, "tab2_plane", offset=3 * word_bytes)
+        w48_plane = zeroed_plane(nc.vector, held, H, "w48_plane")
+        tab_plane = zeroed_plane(nc.gpsimd, tables, T, "tab_plane", offset=3 * word_bytes + T)
+
+        def load_table(source, name, place):
+            return load_words(tables, source.rearrange("p t i -> p (t i)"), T, name, offset=place * word_bytes)
 
         list2 = load_list(offs2, "list2")
-        tab2_w = load_words(tables, tab2_words[0].rearrange("p t i -> p (t i)"), T, "tab2_w", offset=0)
-        load_scale_rows(tab2_plane, 0, tab2_scales[0])
-        w4_raw = load_words(ring, w4_words[0], H // 2, "w4_raw", tag="turned")
+        tab2_w = load_table(tab2_words[0], "tab2_w", 0)
+        w4_raw = load_words(ring, w4_words[0], H // 2, "w4_raw", tag="fw_part", bufs=PART_BUFS)
         w8_raw = load_words(ring, w8_words[0].rearrange("p c i -> p (c i)"), H, "w8_raw", tag="h", bufs=H_BUFS)
+        load_scale_rows(tab2_plane, 0, tab2_scales[0])
+        tab_w = [load_table(tab_words[0], "tab_w0", 1)]
         load_scale_rows(w48_plane, 0, w4_scales[0])
         load_scale_rows(w48_plane, 4, w8_scales[0])
         al_t = load_channel_vector(al, "al_t")
         list1 = load_list(offs, "list1")
-        tab_w = [
-            load_words(tables, tab_words[a].rearrange("p t i -> p (t i)"), T, "tab_w%d" % a, offset=(1 + a) * word_bytes)
-            for a in range(2)
-        ]
+        tab_w.append(load_table(tab_words[1], "tab_w1", 2))
         for q in range(QUADS):
-            nc.scalar.dma_start(
+            nc.gpsimd.dma_start(
                 tab_plane[QUAD * q : QUAD * q + 8, :].bitcast(I32), tab_scales[:, 4 * q : 4 * q + 4, :].bitcast(I32)
             )
-        list4 = load_list(offs4, "list4")
-        list3 = load_list(offs3, "list3")
 
         def load_w1(b):
             raw = ring.tile([P, 2 * PACK * PASS], F32, name="w1_raw", tag="wide", align_bytes=64)
@@ -116,25 +114,24 @@ def tile_list_woven_post_filter_kernel(
             return views
 
         gain2 = [load_gains(wg2, 0, "gain2_0")]
+        list4 = load_list(offs4, "list4")
         w1_raw = [load_w1(0)]
         for t in range(1, PACK):
             gain2.append(load_gains(wg2, t, "gain2_%d" % t))
         gain1 = [load_gains(wg1, 0, "gain1_0")]
+        list3 = load_list(offs3, "list3")
         lo_t = load_channel_vector(lo, "lo_t")
         hi_t = load_channel_vector(hi, "hi_t")
         gain1.append(load_gains(wg1, 1, "gain1_1"))
         gain1.append(load_gains(wg1, 2, "gain1_2"))
         w1_raw.append(load_w1(1))
         gain1.append(load_gains(wg1, 3, "gain1_3"))
-        wd_raw = ring.tile([P, 2, PACK, N], F32, name="wd_raw", tag="codes", align_bytes=64)
+        wd_raw = held.tile([P, 2, PACK, N], F32, name="wd_raw")
         for b in range(2):
             nc.sync.dma_start(wd_raw[:, b, :, :], wd[PASS * b : PASS * (b + 1), :].rearrange("(p j) n -> p j n", j=PACK))
 
-        ident = held.tile([P, P], F32, name="ident")
-        make_identity(nc, ident[:])
-
         rest_t = held.tile([P, 2, PACK], F32, name="rest_t")
-        nc.vector.tensor_scalar(rest_t[:], al_t[:], -1.0, 1.0, ALU.mult, ALU.add)
+        nc.scalar.activation(rest_t[:], al_t[:], COPY, scale=-1.0, bias=1.0)
 
         v2_words = gather(U32, tab2_w, list2, "v2_words")
         v2_plane = gather(U8, tab2_plane, list2, "v2_plane")
@@ -160,7 +157,6 @@ def tile_list_woven_post_filter_kernel(
             for half in range(S // BANK):
                 j = slice(BANK * half, BANK * (half + 1))
                 fw, bw = banks[2 * half], banks[2 * half + 1]
-                turn, back = banks[4 + 2 * half], banks[5 + 2 * half]
                 moving = v2_words[:, j].bitcast(FP8X4)
                 nc.tensor.matmul_mx(
                     fw[:], lhsT=w4[:].bitcast(U8)[:, 2 * P * s : 2 * P * (s + 1)].bitcast(FP4X4), lhsT_scale=w48_scales[:, cols],
@@ -170,23 +166,15 @@ def tile_list_woven_post_filter_kernel(
                     bw[:], lhsT=w8[:, cols].bitcast(FP8X4), lhsT_scale=w48_scales[4:P, cols],
                     rhs=moving, rhs_scale=v2_plane[:, j], start=True, stop=True,
                 )
-                fw_part = ring.tile([P, BANK], F32, name="fw_part", tag="fw_part", bufs=PART_BUFS)
-                bw_part = ring.tile([P, BANK], F32, name="bw_part", tag="bw_part", bufs=PART_BUFS)
-                nc.scalar.activation(fw_part[:], fw[:], COPY, scale=rest_t[:, b, t : t + 1])
-                nc.scalar.activation(bw_part[:], bw[:], COPY, scale=al_t[:, b, t : t + 1])
-                for block in range(BANK // P):
-                    c = slice(P * block, P * (block + 1))
-                    nc.tensor.matmul(turn[:, c], fw_part[:, c], ident[:], is_transpose=True, start=True, stop=False)
-                    nc.tensor.matmul(turn[:, c], bw_part[:, c], ident[:], is_transpose=True, start=False, stop=True)
-                if half in staging:
-                    turned = staging[half]
-                else:
-                    turned = ring.tile([P, BANK], F32, name="turned", tag="turned", align_bytes=64)[:]
-                nc.scalar.copy(turned, turn[:])
-                for block in range(BANK // P):
-                    c = slice(P * block, P * (block + 1))
-                    nc.tensor.transpose(back[:, c], turned[:, c], ident[:])
-                nc.scalar.copy(h2[:, j], back[:])
+                parts = []
+                for name, bank, share in (("fw_part", fw, rest_t), ("bw_part", bw, al_t)):
+                    if (name, half) in staging:
+                        part = staging[name, half]
+                    else:
+                        part = ring.tile([P, BANK], F32, name=name, tag=name, bufs=PART_BUFS, align_bytes=64)[:]
+                    nc.scalar.activation(part, bank[:], COPY, scale=share[:, b, t : t + 1])
+                    parts.append(part)
+                nc.gpsimd.tensor_tensor(h2[:, j], parts[0], parts[1], ALU.add)
 
         def quantise_w1(b, grouped):
             for a in range(2):
@@ -204,7 +192,7 @@ def tile_list_woven_post_filter_kernel(
             codes, plane = w1_mx[b]
             for half in range(S // BANK):
                 j = slice(BANK * half, BANK * (half + 1))
-                bank = banks[7]
+                bank = banks[2 + half]
                 for a in range(2):
                     cols = slice(PASS * a + P * t, PASS * a + P * (t + 1))
                     nc.tensor.matmul_mx(
@@ -231,8 +219,6 @@ def tile_list_woven_post_filter_kernel(
             b, t = divmod(s, PACK)
             return clamped[b][:, T2 * t : T2 * (t + 1)]
 
-        nc.gpsimd.memset(clamped_row(SLICES - 1), 0.0)
-
         def clamp(engine, target, page_part, s):
             b, t = divmod(s, PACK)
             engine.tensor_scalar(target, page_part, hi_t[:, b, t : t + 1], lo_t[:, b, t : t + 1], ALU.min, ALU.max)
@@ -256,61 +242,69 @@ def tile_list_woven_post_filter_kernel(
         def quantise_z(b, source, c0, width):
             nc.vector.quantize_mx(z_codes[b][:, c0 : c0 + width].bitcast(FP8X4), z_plane[b][:, c0 : c0 + width], source)
 
-        def values_tile(before_clamp):
-            if before_clamp is not None:
-                return clamped_row(before_clamp).bitcast(F32)
+        def values_tile():
             return ring.tile([P, S], F32, name="h", tag="h", bufs=H_BUFS, align_bytes=64)[:]
 
-        def put_second(s, staging, before_clamp=None):
-            values = values_tile(before_clamp)
+        def row_as_values(s):
+            return clamped_row(s).bitcast(F32)
+
+        def put_second(s, values, staging):
             blend(s, values, staging)
             put(s, list4, values, gain2[s % PACK])
 
-        def put_first(s, before_clamp=None):
-            values = values_tile(before_clamp)
+        def put_first(s, values):
             features(s, values)
             put(s, list3, values, gain1[s % PACK])
 
+        middle = PACK * T2 // 2
         for s in range(PAGES - 1):
-            put_second(s, {})
+            put_second(s, values_tile(), {})
         w1_grouped = ring.tile([P, 2 * PASS * PACK], BF16, name="w1_grouped0", tag="page", bufs=PAGES, align_bytes=64)
         w1_mx = [quantise_w1(0, w1_grouped)]
-        put_second(3, {})
-        put_first(0)
-        put_first(1, 0)
+        put_second(3, values_tile(), {})
+        put_first(0, values_tile())
+        put_first(1, values_tile())
+        put_first(2, row_as_values(0))
         clamp_page(0)
-        put_first(2, 1)
-        clamp_page(1)
         w1_grouped = ring.tile([P, 2 * PASS * PACK], BF16, name="w1_grouped1", tag="codes", align_bytes=64)
-        put_second(4, {1: bank_view(w1_grouped, PASS * PACK - BANK)}, 2)
+        put_second(4, row_as_values(1), {("bw_part", 1): bank_view(w1_grouped, PASS * PACK - BANK)})
+        clamp_page(1)
+        put_first(3, row_as_values(2))
         clamp_page(2)
-        put_first(3)
         w1_mx.append(quantise_w1(1, w1_grouped))
-        wd_grouped = held.tile([P, 2 * N * PACK], BF16, name="wd_grouped", align_bytes=64)
-        put_second(5, {1: bank_view(wd_grouped, 0)}, 3)
+        put_second(5, row_as_values(SLICES - 1), {})
+        nc.gpsimd.memset(row_as_values(SLICES - 1), 0.0)
+        put_first(4, row_as_values(3))
         clamp_page(3)
-        put_first(4)
+        woven = [ring.tile([P, PACK * T2], BF16, name="woven%d" % b, tag="wide", align_bytes=64) for b in range(2)]
+        put_second(6, values_tile(), {("bw_part", 1): bank_view(woven[0], 0)})
+        put_first(5, row_as_values(4))
+        clamp_page(4)
+        weave(0, 0)
+        z_codes[0] = ring.tile([P, T2], U32, name="z_codes0", tag="codes", align_bytes=64)
+        quantise_z(0, woven[0][:, :middle], 0, T2 // 2)
+        put_first(6, woven[0][:, middle : middle + 2 * S].bitcast(F32))
+        put_first(7, row_as_values(5))
+        clamp_page(5)
+        weave(0, 1)
+        quantise_z(0, woven[0][:, middle:], T2 // 2, T2 // 2)
+        wd_grouped = held.tile([P, 2 * N * PACK], BF16, name="wd_grouped", align_bytes=64)
+        put_second(
+            7,
+            values_tile(),
+            {
+                ("bw_part", 0): bank_view(wd_grouped, 0),
+                ("fw_part", 1): row_as_values(6)[:, :BANK],
+                ("bw_part", 1): bank_view(woven[1], middle - BANK),
+            },
+        )
         nc.scalar.copy(
             wd_grouped[:].rearrange("p (b n j) -> p b n j", b=2, j=PACK), wd_raw[:].rearrange("p b j n -> p b n j")
         )
         wd_codes = held.tile([P, 2 * N], U32, name="wd_codes", align_bytes=64)
         wd_plane = held.tile([P, 2 * N], U8, name="wd_plane", align_bytes=64)
         nc.vector.quantize_mx(wd_codes[:].bitcast(FP8X4), wd_plane[:], wd_grouped[:])
-        middle = PACK * T2 // 2
-        woven = [ring.tile([P, PACK * T2], BF16, name="woven%d" % b, tag="wide", align_bytes=64) for b in range(2)]
-        put_second(6, {1: bank_view(woven[0], 0)}, 4)
-        clamp_page(4)
-        put_first(5)
-        weave(0, 0)
-        z_codes[0] = ring.tile([P, T2], U32, name="z_codes0", tag="codes", align_bytes=64)
-        quantise_z(0, woven[0][:, :middle], 0, T2 // 2)
-        put_first(6, 5)
-        clamp_page(5)
-        put_first(7, 6)
         clamp_page(6)
-        put_second(7, {0: bank_view(woven[0], middle), 1: bank_view(woven[1], middle - BANK)})
-        weave(0, 1)
-        quantise_z(0, woven[0][:, middle:], T2 // 2, T2 // 2)
         for half in range(2):
             weave(1, half)
 
@@ -346,7 +340,7 @@ def tile_list_woven_post_filter_kernel(
             quantise_z(1, piece(chunk), BANK * chunk, BANK)
             filter_pass(1, chunk)
             for n in range(N // P):
-                result = ring.tile([P, BANK], F32, name="result", tag=("fw_part", "bw_part")[n], bufs=PART_BUFS)
+                result = ring.tile([P, BANK], F32, name="result", tag=("fw_part", "bw_part")[n], bufs=PART_BUFS, align_bytes=64)
                 if chunk == chunks - 1 and n == 1:
                     nc.vector.tensor_copy(result[:], banks[2 * chunk + n][:])
                 else:

@@ -25,7 +25,7 @@ QUAD = 32
 SLICES = H // P
 H_BUFS = 2
 PAGES = 4
-PART_BUFS = 4
+PART_BUFS = 5
 
 
 def tile_list_woven_post_filter_kernel(
@@ -70,7 +70,7 @@ def tile_list_woven_post_filter_kernel(
         def load_gains(source, t, name):
             tile = held.tile([P, S], F32, name=name)
             rows = source.rearrange("(q t) j -> q t j", t=PACK)
-            for q in range(QUADS):
+            for q in (0, 2, 1, 3):
                 nc.sync.dma_start(tile[QUAD * q : QUAD * (q + 1), :], rows[:, t, :])
             return tile
 
@@ -87,14 +87,14 @@ def tile_list_woven_post_filter_kernel(
         def load_table(source, name, place):
             return load_words(tables, source.rearrange("p t i -> p (t i)"), T, name, offset=place * word_bytes)
 
-        list2 = load_list(offs2, "list2")
-        tab2_w = load_table(tab2_words[0], "tab2_w", 0)
         w4_raw = load_words(ring, w4_words[0], H // 2, "w4_raw", tag="fw_part", bufs=PART_BUFS)
         w8_raw = load_words(ring, w8_words[0].rearrange("p c i -> p (c i)"), H, "w8_raw", tag="h", bufs=H_BUFS)
+        list2 = load_list(offs2, "list2")
         load_scale_rows(tab2_plane, 0, tab2_scales[0])
-        tab_w = [load_table(tab_words[0], "tab_w0", 1)]
+        tab2_w = load_table(tab2_words[0], "tab2_w", 0)
         load_scale_rows(w48_plane, 0, w4_scales[0])
         load_scale_rows(w48_plane, 4, w8_scales[0])
+        tab_w = [load_table(tab_words[0], "tab_w0", 1)]
         al_t = load_channel_vector(al, "al_t")
         list1 = load_list(offs, "list1")
         tab_w.append(load_table(tab_words[1], "tab_w1", 2))
@@ -115,8 +115,9 @@ def tile_list_woven_post_filter_kernel(
 
         gain2 = [load_gains(wg2, 0, "gain2_0")]
         list4 = load_list(offs4, "list4")
+        gain2.append(load_gains(wg2, 1, "gain2_1"))
         w1_raw = [load_w1(0)]
-        for t in range(1, PACK):
+        for t in range(2, PACK):
             gain2.append(load_gains(wg2, t, "gain2_%d" % t))
         gain1 = [load_gains(wg1, 0, "gain1_0")]
         list3 = load_list(offs3, "list3")
@@ -133,9 +134,6 @@ def tile_list_woven_post_filter_kernel(
         rest_t = held.tile([P, 2, PACK], F32, name="rest_t")
         nc.scalar.activation(rest_t[:], al_t[:], COPY, scale=-1.0, bias=1.0)
 
-        v2_words = gather(U32, tab2_w, list2, "v2_words")
-        v2_plane = gather(U8, tab2_plane, list2, "v2_plane")
-
         def reorder_columns(dtype, source, name, columns):
             tile = held.tile([P, columns], source.dtype, name=name, align_bytes=64)
             nc.vector.tensor_copy(
@@ -146,35 +144,36 @@ def tile_list_woven_post_filter_kernel(
 
         w4 = reorder_columns(U16, w4_raw, "w4", H // 2)
         w8 = reorder_columns(U32, w8_raw, "w8", H)
+        v2_plane = gather(U8, tab2_plane, list2, "v2_plane")
+        v2_words = gather(U32, tab2_w, list2, "v2_words")
         w48_scales = reorder_columns(U8, w48_plane, "w48_scales", H)
 
         v_words = [gather(U32, tab_w[a], list1, "v_words%d" % a) for a in range(2)]
         v_plane = gather(U8, tab_plane, list1, "v_plane")
 
-        def blend(s, h2, staging):
+        def blend(s, half, h2, staging):
             b, t = divmod(s, PACK)
             cols = slice(P * s, P * (s + 1))
-            for half in range(S // BANK):
-                j = slice(BANK * half, BANK * (half + 1))
-                fw, bw = banks[2 * half], banks[2 * half + 1]
-                moving = v2_words[:, j].bitcast(FP8X4)
-                nc.tensor.matmul_mx(
-                    fw[:], lhsT=w4[:].bitcast(U8)[:, 2 * P * s : 2 * P * (s + 1)].bitcast(FP4X4), lhsT_scale=w48_scales[:, cols],
-                    rhs=moving, rhs_scale=v2_plane[:, j], start=True, stop=True,
-                )
-                nc.tensor.matmul_mx(
-                    bw[:], lhsT=w8[:, cols].bitcast(FP8X4), lhsT_scale=w48_scales[4:P, cols],
-                    rhs=moving, rhs_scale=v2_plane[:, j], start=True, stop=True,
-                )
-                parts = []
-                for name, bank, share in (("fw_part", fw, rest_t), ("bw_part", bw, al_t)):
-                    if (name, half) in staging:
-                        part = staging[name, half]
-                    else:
-                        part = ring.tile([P, BANK], F32, name=name, tag=name, bufs=PART_BUFS, align_bytes=64)[:]
-                    nc.scalar.activation(part, bank[:], COPY, scale=share[:, b, t : t + 1])
-                    parts.append(part)
-                nc.gpsimd.tensor_tensor(h2[:, j], parts[0], parts[1], ALU.add)
+            j = slice(BANK * half, BANK * (half + 1))
+            fw, bw = banks[2 * half], banks[2 * half + 1]
+            moving = v2_words[:, j].bitcast(FP8X4)
+            nc.tensor.matmul_mx(
+                fw[:], lhsT=w4[:].bitcast(U8)[:, 2 * P * s : 2 * P * (s + 1)].bitcast(FP4X4), lhsT_scale=w48_scales[:, cols],
+                rhs=moving, rhs_scale=v2_plane[:, j], start=True, stop=True,
+            )
+            nc.tensor.matmul_mx(
+                bw[:], lhsT=w8[:, cols].bitcast(FP8X4), lhsT_scale=w48_scales[4:P, cols],
+                rhs=moving, rhs_scale=v2_plane[:, j], start=True, stop=True,
+            )
+            parts = []
+            for name, bank, share in (("fw_part", fw, rest_t), ("bw_part", bw, al_t)):
+                if (name, half) in staging:
+                    part = staging[name, half]
+                else:
+                    part = ring.tile([P, BANK], F32, name=name, tag=name, bufs=PART_BUFS, align_bytes=64)[:]
+                nc.scalar.activation(part, bank[:], COPY, scale=share[:, b, t : t + 1])
+                parts.append(part)
+            nc.gpsimd.tensor_tensor(h2[:, j], parts[0], parts[1], ALU.add)
 
         def quantise_w1(b, grouped):
             for a in range(2):
@@ -204,12 +203,13 @@ def tile_list_woven_post_filter_kernel(
 
         pages = {}
 
-        def put(s, offsets, values, gains):
+        def put(s, offsets, values, gains, first, count):
             if s not in pages:
                 pages[s] = ring.tile([P, T2], F32, name="page", tag="page", bufs=PAGES, align_bytes=64)
-            weighted = ring.tile([P, S], F32, name="weighted", tag="weighted", bufs=3)
-            nc.gpsimd.tensor_tensor(weighted[:], values, gains[:], ALU.mult)
-            nc.vector.tensor_copy(pages[s][:].indirect(offsets[:]), weighted[:])
+            j = slice(first, first + count)
+            weighted = ring.tile([P, count], F32, name="weighted", tag="weighted", bufs=3)
+            nc.gpsimd.tensor_tensor(weighted[:], values[:, j], gains[:, j], ALU.mult)
+            nc.vector.tensor_copy(pages[s][:].indirect(offsets[:, first // 16 : (first + count) // 16]), weighted[:])
 
         clamped = [
             tables.tile([P, PACK * T2], BF16, name="clamped%d" % b, offset=2 * PACK * T2 * b, align_bytes=64) for b in range(2)
@@ -249,12 +249,16 @@ def tile_list_woven_post_filter_kernel(
             return clamped_row(s).bitcast(F32)
 
         def put_second(s, values, staging):
-            blend(s, values, staging)
-            put(s, list4, values, gain2[s % PACK])
+            for half in range(S // BANK):
+                blend(s, half, values, staging)
+                if s == 0:
+                    put(s, list4, values, gain2[0], BANK * half, BANK)
+            if s > 0:
+                put(s, list4, values, gain2[s % PACK], 0, S)
 
         def put_first(s, values):
             features(s, values)
-            put(s, list3, values, gain1[s % PACK])
+            put(s, list3, values, gain1[s % PACK], 0, S)
 
         middle = PACK * T2 // 2
         for s in range(PAGES - 1):
@@ -310,39 +314,47 @@ def tile_list_woven_post_filter_kernel(
 
         z_codes[1] = ring.tile([P, T2], U32, name="z_codes1", tag="codes", align_bytes=64)
 
+        chunks = [(0, BANK), (BANK, BANK), (2 * BANK, BANK), (3 * BANK, BANK // 2), (3 * BANK + BANK // 2, BANK // 2)]
+
+        def sums(chunk, n):
+            return banks[(2 * chunk + n) % len(banks)][:, : chunks[chunk][1]]
+
         def filter_pass(b, chunk):
-            cols = slice(BANK * chunk, BANK * (chunk + 1))
+            first, width = chunks[chunk]
+            cols = slice(first, first + width)
             for n in range(N // P):
                 w_cols = slice(N * b + P * n, N * b + P * (n + 1))
                 nc.tensor.matmul_mx(
-                    banks[2 * chunk + n][:], lhsT=wd_codes[:, w_cols].bitcast(FP8X4), lhsT_scale=wd_plane[:, w_cols],
+                    sums(chunk, n), lhsT=wd_codes[:, w_cols].bitcast(FP8X4), lhsT_scale=wd_plane[:, w_cols],
                     rhs=z_codes[b][:, cols].bitcast(FP8X4), rhs_scale=z_plane[b][:, cols],
                     start=(b == 0), stop=(b == 1),
                 )
 
-        for chunk in range(T2 // BANK):
-            filter_pass(0, chunk)
         last = SLICES - 1
-        chunks = T2 // BANK
 
         def piece(chunk):
-            return woven[1][:, chunk * PACK * BANK : (chunk + 1) * PACK * BANK]
+            first, width = chunks[chunk]
+            return woven[1][:, PACK * first : PACK * (first + width)]
 
         def clamp_last(chunk):
+            first, width = chunks[chunk]
             target = piece(chunk).rearrange("p (c t) -> p c t", t=PACK)[:, :, PACK - 1]
-            clamp(nc.vector, target, pages[last][:, BANK * chunk : BANK * (chunk + 1)], last)
+            clamp(nc.vector, target, pages[last][:, first : first + width], last)
 
+        for chunk in range(len(banks) // 2):
+            filter_pass(0, chunk)
         clamp_last(0)
-        for chunk in range(chunks):
-            cols = slice(BANK * chunk, BANK * (chunk + 1))
-            if chunk + 1 < chunks:
+        for chunk, (first, width) in enumerate(chunks):
+            if chunk + 1 < len(chunks):
                 clamp_last(chunk + 1)
-            quantise_z(1, piece(chunk), BANK * chunk, BANK)
+            quantise_z(1, piece(chunk), first, width)
+            if chunk >= len(banks) // 2:
+                filter_pass(0, chunk)
             filter_pass(1, chunk)
             for n in range(N // P):
-                result = ring.tile([P, BANK], F32, name="result", tag=("fw_part", "bw_part")[n], bufs=PART_BUFS, align_bytes=64)
-                if chunk == chunks - 1 and n == 1:
-                    nc.vector.tensor_copy(result[:], banks[2 * chunk + n][:])
+                result = ring.tile([P, width], F32, name="result", tag=("fw_part", "bw_part")[n], bufs=PART_BUFS, align_bytes=64)
+                if chunk >= len(chunks) - 2 and n == 1:
+                    nc.vector.tensor_copy(result[:], sums(chunk, n))
                 else:
-                    nc.scalar.copy(result[:], banks[2 * chunk + n][:])
-                nc.sync.dma_start(out[P * n : P * (n + 1), cols], result[:])
+                    nc.scalar.copy(result[:], sums(chunk, n))
+                nc.sync.dma_start(out[P * n : P * (n + 1), first : first + width], result[:])

from contextlib import ExitStack

import concourse.mybir as mybir

F32 = mybir.dt.float32
BF16 = mybir.dt.bfloat16
I32 = mybir.dt.int32
U32 = mybir.dt.uint32
U16 = mybir.dt.uint16
U8 = mybir.dt.uint8
FP8X4 = mybir.dt.float8_e4m3fn_x4
FP4X4 = mybir.dt.float4_e2m1fn_x4
ALU = mybir.AluOpType
COPY = mybir.ActivationFunctionType.Copy

K, K2, H, N, T, S, T2 = 1024, 512, 1024, 256, 2048, 1024, 2048
FLOPS = 2 * (K * H * S + 2 * K2 * H * S + H * N * T2)

P = 128
PACK = 4
PASS = P * PACK
BANK = 512
QUADS = 4
QUAD = 32
SLICES = H // P
H_BUFS = 2
PAGES = 4
PART_BUFS = 5


def tile_list_woven_post_filter_kernel(
    tc, tab_words, tab_scales, tab2_words, tab2_scales, offs, offs2, offs3, offs4,
    w1, w4_words, w4_scales, w8_words, w8_scales, al, wg1, wg2, lo, hi, wd, out,
):
    nc = tc.nc
    with ExitStack() as ctx:
        lists = ctx.enter_context(tc.tile_pool(name="lists", bufs=1))
        held = ctx.enter_context(tc.tile_pool(name="held", bufs=1))
        tables = ctx.enter_context(tc.tile_pool(name="tables", bufs=1))
        ring = ctx.enter_context(tc.tile_pool(name="ring", bufs=2))
        psum = ctx.enter_context(tc.psum_pool(name="psum", bufs=1))

        banks = [psum.tile([P, BANK], F32, name="bank%d" % i) for i in range(8)]

        def load_list(source, name):
            tile = lists.tile([P, S // 16], U16, name=name)
            nc.sync.dma_start(tile[:], source)
            return tile

        def load_words(pool, source, columns, name, **where):
            tile = pool.tile([P, columns], I32, name=name, align_bytes=64, **where)
            nc.sync.dma_start(tile[:], source.bitcast(I32))
            return tile

        def zeroed_plane(engine, pool, columns, name, **where):
            tile = pool.tile([P, columns], U8, name=name, align_bytes=64, **where)
            engine.memset(tile[:].bitcast(I32), 0)
            return tile

        def load_scale_rows(plane, first_row, source):
            for q in range(QUADS):
                row = QUAD * q + first_row
                nc.sync.dma_start(plane[row : row + 4, :].bitcast(I32), source[4 * q : 4 * q + 4, :].bitcast(I32))

        def load_channel_vector(source, name):
            tile = held.tile([P, 2, PACK], F32, name=name)
            nc.sync.dma_start(tile[:], source.rearrange("(b p t) -> p b t", p=P, t=PACK))
            return tile

        def load_gains(source, t, name):
            tile = held.tile([P, S], F32, name=name)
            rows = source.rearrange("(q t) j -> q t j", t=PACK)
            for q in (0, 2, 1, 3):
                nc.sync.dma_start(tile[QUAD * q : QUAD * (q + 1), :], rows[:, t, :])
            return tile

        def gather(dtype, table, offsets, name):
            tile = held.tile([P, S], dtype, name=name, align_bytes=64)
            nc.vector.tensor_copy(tile[:], table[:].bitcast(dtype).indirect(offsets[:]))
            return tile

        word_bytes = 4 * T
        tab2_plane = zeroed_plane(nc.gpsimd, tables, T, "tab2_plane", offset=3 * word_bytes)
        w48_plane = zeroed_plane(nc.vector, held, H, "w48_plane")
        tab_plane = zeroed_plane(nc.gpsimd, tables, T, "tab_plane", offset=3 * word_bytes + T)

        def load_table(source, name, place):
            return load_words(tables, source.rearrange("p t i -> p (t i)"), T, name, offset=place * word_bytes)

        w4_raw = load_words(ring, w4_words[0], H // 2, "w4_raw", tag="fw_part", bufs=PART_BUFS)
        w8_raw = load_words(ring, w8_words[0].rearrange("p c i -> p (c i)"), H, "w8_raw", tag="h", bufs=H_BUFS)
        list2 = load_list(offs2, "list2")
        load_scale_rows(tab2_plane, 0, tab2_scales[0])
        tab2_w = load_table(tab2_words[0], "tab2_w", 0)
        load_scale_rows(w48_plane, 0, w4_scales[0])
        load_scale_rows(w48_plane, 4, w8_scales[0])
        tab_w = [load_table(tab_words[0], "tab_w0", 1)]
        al_t = load_channel_vector(al, "al_t")
        list1 = load_list(offs, "list1")
        tab_w.append(load_table(tab_words[1], "tab_w1", 2))
        for q in range(QUADS):
            nc.gpsimd.dma_start(
                tab_plane[QUAD * q : QUAD * q + 8, :].bitcast(I32), tab_scales[:, 4 * q : 4 * q + 4, :].bitcast(I32)
            )

        def load_w1(b):
            raw = ring.tile([P, 2 * PACK * PASS], F32, name="w1_raw", tag="wide", align_bytes=64)
            views = []
            for a in range(2):
                view = raw[:, a * PACK * PASS : (a + 1) * PACK * PASS].rearrange("p (j c) -> p j c", j=PACK)
                rows = w1[PASS * a : PASS * (a + 1), PASS * b : PASS * (b + 1)]
                nc.sync.dma_start(view, rows.rearrange("(p j) c -> p j c", j=PACK))
                views.append(view)
            return views

        gain2 = [load_gains(wg2, 0, "gain2_0")]
        list4 = load_list(offs4, "list4")
        gain2.append(load_gains(wg2, 1, "gain2_1"))
        w1_raw = [load_w1(0)]
        for t in range(2, PACK):
            gain2.append(load_gains(wg2, t, "gain2_%d" % t))
        gain1 = [load_gains(wg1, 0, "gain1_0")]
        list3 = load_list(offs3, "list3")
        lo_t = load_channel_vector(lo, "lo_t")
        hi_t = load_channel_vector(hi, "hi_t")
        gain1.append(load_gains(wg1, 1, "gain1_1"))
        gain1.append(load_gains(wg1, 2, "gain1_2"))
        w1_raw.append(load_w1(1))
        gain1.append(load_gains(wg1, 3, "gain1_3"))
        wd_raw = held.tile([P, 2, PACK, N], F32, name="wd_raw")
        for b in range(2):
            nc.sync.dma_start(wd_raw[:, b, :, :], wd[PASS * b : PASS * (b + 1), :].rearrange("(p j) n -> p j n", j=PACK))

        rest_t = held.tile([P, 2, PACK], F32, name="rest_t")
        nc.scalar.activation(rest_t[:], al_t[:], COPY, scale=-1.0, bias=1.0)

        def reorder_columns(dtype, source, name, columns):
            tile = held.tile([P, columns], source.dtype, name=name, align_bytes=64)
            nc.vector.tensor_copy(
                tile[:].bitcast(dtype).rearrange("p (b t c i) -> p b c t i", b=2, t=PACK, i=4),
                source[:].bitcast(dtype).rearrange("p (b c i t) -> p b c t i", b=2, t=PACK, i=4),
            )
            return tile

        w4 = reorder_columns(U16, w4_raw, "w4", H // 2)
        w8 = reorder_columns(U32, w8_raw, "w8", H)
        v2_plane = gather(U8, tab2_plane, list2, "v2_plane")
        v2_words = gather(U32, tab2_w, list2, "v2_words")
        w48_scales = reorder_columns(U8, w48_plane, "w48_scales", H)

        v_words = [gather(U32, tab_w[a], list1, "v_words%d" % a) for a in range(2)]
        v_plane = gather(U8, tab_plane, list1, "v_plane")

        def blend(s, half, h2, staging):
            b, t = divmod(s, PACK)
            cols = slice(P * s, P * (s + 1))
            j = slice(BANK * half, BANK * (half + 1))
            fw, bw = banks[2 * half], banks[2 * half + 1]
            moving = v2_words[:, j].bitcast(FP8X4)
            nc.tensor.matmul_mx(
                fw[:], lhsT=w4[:].bitcast(U8)[:, 2 * P * s : 2 * P * (s + 1)].bitcast(FP4X4), lhsT_scale=w48_scales[:, cols],
                rhs=moving, rhs_scale=v2_plane[:, j], start=True, stop=True,
            )
            nc.tensor.matmul_mx(
                bw[:], lhsT=w8[:, cols].bitcast(FP8X4), lhsT_scale=w48_scales[4:P, cols],
                rhs=moving, rhs_scale=v2_plane[:, j], start=True, stop=True,
            )
            parts = []
            for name, bank, share in (("fw_part", fw, rest_t), ("bw_part", bw, al_t)):
                if (name, half) in staging:
                    part = staging[name, half]
                else:
                    part = ring.tile([P, BANK], F32, name=name, tag=name, bufs=PART_BUFS, align_bytes=64)[:]
                nc.scalar.activation(part, bank[:], COPY, scale=share[:, b, t : t + 1])
                parts.append(part)
            nc.gpsimd.tensor_tensor(h2[:, j], parts[0], parts[1], ALU.add)

        def quantise_w1(b, grouped):
            for a in range(2):
                nc.scalar.copy(
                    grouped[:, a * PASS * PACK : (a + 1) * PASS * PACK].rearrange("p (t m j) -> p m t j", t=PACK, j=PACK),
                    w1_raw[b][a].rearrange("p j (m t) -> p m t j", t=PACK),
                )
            codes = held.tile([P, 2 * PASS], U32, name="w1_codes%d" % b, align_bytes=64)
            plane = held.tile([P, 2 * PASS], U8, name="w1_plane%d" % b, align_bytes=64)
            nc.vector.quantize_mx(codes[:].bitcast(FP8X4), plane[:], grouped[:])
            return codes, plane

        def features(s, h1):
            b, t = divmod(s, PACK)
            codes, plane = w1_mx[b]
            for half in range(S // BANK):
                j = slice(BANK * half, BANK * (half + 1))
                bank = banks[2 + half]
                for a in range(2):
                    cols = slice(PASS * a + P * t, PASS * a + P * (t + 1))
                    nc.tensor.matmul_mx(
                        bank[:], lhsT=codes[:, cols].bitcast(FP8X4), lhsT_scale=plane[:, cols],
                        rhs=v_words[a][:, j].bitcast(FP8X4), rhs_scale=v_plane[4 * a : P, j],
                        start=(a == 0), stop=(a == 1),
                    )
                nc.scalar.copy(h1[:, j], bank[:])

        pages = {}

        def put(s, offsets, values, gains, first, count):
            if s not in pages:
                pages[s] = ring.tile([P, T2], F32, name="page", tag="page", bufs=PAGES, align_bytes=64)
            j = slice(first, first + count)
            weighted = ring.tile([P, count], F32, name="weighted", tag="weighted", bufs=3)
            nc.gpsimd.tensor_tensor(weighted[:], values[:, j], gains[:, j], ALU.mult)
            nc.vector.tensor_copy(pages[s][:].indirect(offsets[:, first // 16 : (first + count) // 16]), weighted[:])

        clamped = [
            tables.tile([P, PACK * T2], BF16, name="clamped%d" % b, offset=2 * PACK * T2 * b, align_bytes=64) for b in range(2)
        ]

        def clamped_row(s):
            b, t = divmod(s, PACK)
            return clamped[b][:, T2 * t : T2 * (t + 1)]

        def clamp(engine, target, page_part, s):
            b, t = divmod(s, PACK)
            engine.tensor_scalar(target, page_part, hi_t[:, b, t : t + 1], lo_t[:, b, t : t + 1], ALU.min, ALU.max)

        def clamp_page(s):
            clamp(nc.gpsimd, clamped_row(s), pages[s][:], s)

        def weave(b, half):
            c0 = half * T2 // 2
            nc.scalar.copy(
                woven[b][:, PACK * c0 : PACK * (c0 + T2 // 2)].rearrange("p (c i t) -> p c t i", t=PACK, i=4),
                clamped[b][:].rearrange("p (t c) -> p t c", t=PACK)[:, :, c0 : c0 + T2 // 2].rearrange("p t (c i) -> p c t i", i=4),
            )

        def bank_view(tile, first):
            return tile[:, first : first + 2 * BANK].bitcast(F32)

        z_codes = [None, None]
        z_plane = [held.tile([P, T2], U8, name="z_plane%d" % b, align_bytes=64) for b in range(2)]

        def quantise_z(b, source, c0, width):
            nc.vector.quantize_mx(z_codes[b][:, c0 : c0 + width].bitcast(FP8X4), z_plane[b][:, c0 : c0 + width], source)

        def values_tile():
            return ring.tile([P, S], F32, name="h", tag="h", bufs=H_BUFS, align_bytes=64)[:]

        def row_as_values(s):
            return clamped_row(s).bitcast(F32)

        def put_second(s, values, staging):
            for half in range(S // BANK):
                blend(s, half, values, staging)
                if s == 0:
                    put(s, list4, values, gain2[0], BANK * half, BANK)
            if s > 0:
                put(s, list4, values, gain2[s % PACK], 0, S)

        def put_first(s, values):
            features(s, values)
            put(s, list3, values, gain1[s % PACK], 0, S)

        middle = PACK * T2 // 2
        for s in range(PAGES - 1):
            put_second(s, values_tile(), {})
        w1_grouped = ring.tile([P, 2 * PASS * PACK], BF16, name="w1_grouped0", tag="page", bufs=PAGES, align_bytes=64)
        w1_mx = [quantise_w1(0, w1_grouped)]
        put_second(3, values_tile(), {})
        put_first(0, values_tile())
        put_first(1, values_tile())
        put_first(2, row_as_values(0))
        clamp_page(0)
        w1_grouped = ring.tile([P, 2 * PASS * PACK], BF16, name="w1_grouped1", tag="codes", align_bytes=64)
        put_second(4, row_as_values(1), {("bw_part", 1): bank_view(w1_grouped, PASS * PACK - BANK)})
        clamp_page(1)
        put_first(3, row_as_values(2))
        clamp_page(2)
        w1_mx.append(quantise_w1(1, w1_grouped))
        put_second(5, row_as_values(SLICES - 1), {})
        nc.gpsimd.memset(row_as_values(SLICES - 1), 0.0)
        put_first(4, row_as_values(3))
        clamp_page(3)
        woven = [ring.tile([P, PACK * T2], BF16, name="woven%d" % b, tag="wide", align_bytes=64) for b in range(2)]
        put_second(6, values_tile(), {("bw_part", 1): bank_view(woven[0], 0)})
        put_first(5, row_as_values(4))
        clamp_page(4)
        weave(0, 0)
        z_codes[0] = ring.tile([P, T2], U32, name="z_codes0", tag="codes", align_bytes=64)
        quantise_z(0, woven[0][:, :middle], 0, T2 // 2)
        put_first(6, woven[0][:, middle : middle + 2 * S].bitcast(F32))
        put_first(7, row_as_values(5))
        clamp_page(5)
        weave(0, 1)
        quantise_z(0, woven[0][:, middle:], T2 // 2, T2 // 2)
        wd_grouped = held.tile([P, 2 * N * PACK], BF16, name="wd_grouped", align_bytes=64)
        put_second(
            7,
            values_tile(),
            {
                ("bw_part", 0): bank_view(wd_grouped, 0),
                ("fw_part", 1): row_as_values(6)[:, :BANK],
                ("bw_part", 1): bank_view(woven[1], middle - BANK),
            },
        )
        nc.scalar.copy(
            wd_grouped[:].rearrange("p (b n j) -> p b n j", b=2, j=PACK), wd_raw[:].rearrange("p b j n -> p b n j")
        )
        wd_codes = held.tile([P, 2 * N], U32, name="wd_codes", align_bytes=64)
        wd_plane = held.tile([P, 2 * N], U8, name="wd_plane", align_bytes=64)
        nc.vector.quantize_mx(wd_codes[:].bitcast(FP8X4), wd_plane[:], wd_grouped[:])
        clamp_page(6)
        for half in range(2):
            weave(1, half)

        z_codes[1] = ring.tile([P, T2], U32, name="z_codes1", tag="codes", align_bytes=64)

        chunks = [(0, BANK), (BANK, BANK), (2 * BANK, BANK), (3 * BANK, BANK // 2), (3 * BANK + BANK // 2, BANK // 2)]

        def sums(chunk, n):
            return banks[(2 * chunk + n) % len(banks)][:, : chunks[chunk][1]]

        def filter_pass(b, chunk):
            first, width = chunks[chunk]
            cols = slice(first, first + width)
            for n in range(N // P):
                w_cols = slice(N * b + P * n, N * b + P * (n + 1))
                nc.tensor.matmul_mx(
                    sums(chunk, n), lhsT=wd_codes[:, w_cols].bitcast(FP8X4), lhsT_scale=wd_plane[:, w_cols],
                    rhs=z_codes[b][:, cols].bitcast(FP8X4), rhs_scale=z_plane[b][:, cols],
                    start=(b == 0), stop=(b == 1),
                )

        last = SLICES - 1

        def piece(chunk):
            first, width = chunks[chunk]
            return woven[1][:, PACK * first : PACK * (first + width)]

        def clamp_last(chunk):
            first, width = chunks[chunk]
            target = piece(chunk).rearrange("p (c t) -> p c t", t=PACK)[:, :, PACK - 1]
            clamp(nc.vector, target, pages[last][:, first : first + width], last)

        for chunk in range(len(banks) // 2):
            filter_pass(0, chunk)
        clamp_last(0)
        for chunk, (first, width) in enumerate(chunks):
            if chunk + 1 < len(chunks):
                clamp_last(chunk + 1)
            quantise_z(1, piece(chunk), first, width)
            if chunk >= len(banks) // 2:
                filter_pass(0, chunk)
            filter_pass(1, chunk)
            for n in range(N // P):
                result = ring.tile([P, width], F32, name="result", tag=("fw_part", "bw_part")[n], bufs=PART_BUFS, align_bytes=64)
                if chunk >= len(chunks) - 2 and n == 1:
                    nc.vector.tensor_copy(result[:], sums(chunk, n))
                else:
                    nc.scalar.copy(result[:], sums(chunk, n))
                nc.sync.dma_start(out[P * n : P * (n + 1), first : first + width], result[:])
